import numpy as np
import ml_dtypes


def mxq(x, axis, fmt="e4m3"):
    dtype, down = {"e4m3": (ml_dtypes.float8_e4m3fn, 7), "e5m2": (ml_dtypes.float8_e5m2, 14)}[fmt]
    v = np.moveaxis(np.asarray(x, np.float32).astype(ml_dtypes.bfloat16).astype(np.float64), axis, -1)
    blocks = v.reshape(v.shape[:-1] + (-1, 32))
    amax = np.abs(blocks).max(-1, keepdims=True)
    byte = np.maximum(np.where(amax > 0, np.frexp(amax)[1] - 1 + 127, 0) - down, 1)
    scale = np.exp2(byte - 127.0)
    codes = (blocks / scale).astype(np.float32).astype(dtype).astype(np.float64)
    return np.moveaxis((codes * scale).reshape(v.shape), -1, axis)


WIDE = False


def mx_kscale(k):
    if not WIDE:
        return np.ones(k)
    levels = np.array([30, -30])
    if k % 512:
        return np.exp2(np.random.permutation(np.resize(levels, k // 32))).repeat(32)
    a = np.empty((k // 512, 16))
    for p in range(k // 512):
        a[p, :8] = np.random.permutation(np.resize(levels, 8))
        for g in range(8):
            far = levels[np.abs(levels - a[p, g]) >= 10]
            a[p, g + 8] = far[np.random.randint(len(far))]
    return np.exp2(a.ravel()).repeat(32)


def f64(x):
    return np.asarray(x).astype(np.float64)


def striped(idx):
    return np.tile(np.asarray(idx).reshape(-1, 16).T, (8, 1)).astype(np.uint16)


def unstriped(offs):
    return offs[:16].T.reshape(-1).astype(np.int64)


E2M1 = np.array([0.0, 0.5, 1.0, 1.5, 2.0, 3.0, 4.0, 6.0, -0.0, -0.5, -1.0, -1.5, -2.0, -3.0, -4.0, -6.0])


def pack_weight(w, fmt):
    k, n = w.shape
    w = f64(np.asarray(w, np.float32).astype(ml_dtypes.bfloat16)).reshape(k // 32, 32, n)
    amax = np.abs(w).max(1)
    if fmt in ("e4m3", "e5m2"):
        byte = np.frexp(amax)[1] - 1 + 127 - (7 if fmt == "e4m3" else 14)
    else:
        mant, ex = np.frexp(amax / 6.0)
        byte = np.where(mant > 0.5, ex, ex - 1) + 127
    byte = np.clip(np.where(amax > 0, byte, 1), 1, 254)
    scaled = (w * np.exp2(127.0 - byte)[:, None, :]).reshape(k, n).astype(np.float32)
    by_word = np.ascontiguousarray(scaled.reshape(k // 512, 128, 4, n).transpose(0, 1, 3, 2))
    if fmt in ("e4m3", "e5m2"):
        words = by_word.astype(ml_dtypes.float8_e4m3fn if fmt == "e4m3" else ml_dtypes.float8_e5m2).view(np.uint8)
    else:
        c = by_word.astype(ml_dtypes.float4_e2m1fn).view(np.uint8) & 0xF
        words = (c[..., 0::2] | (c[..., 1::2] << 4)).reshape(k // 512, 128, 2 * n)
    return np.ascontiguousarray(words), np.ascontiguousarray(byte.astype(np.uint8).reshape(k // 512, 16, n))


def unpack_weight(words, scales, fmt):
    g, _, n = scales.shape
    words = np.ascontiguousarray(words).reshape(g, 128, n, -1)
    if fmt in ("e4m3", "e5m2"):
        vals = words.view(ml_dtypes.float8_e4m3fn if fmt == "e4m3" else ml_dtypes.float8_e5m2).astype(np.float64)
    else:
        nib = np.empty((g, 128, n, 4), np.uint8)
        nib[..., 0::2] = words & 0xF
        nib[..., 1::2] = words >> 4
        vals = E2M1[nib]
    vals = vals * np.repeat(np.exp2(scales.astype(np.float64) - 127.0), 8, axis=1)[..., None]
    return vals.transpose(0, 1, 3, 2).reshape(g * 512, n)


def bf(x):
    return np.asarray(x, np.float32).astype(ml_dtypes.bfloat16)


def planes(Y):
    r, m = Y.shape
    b = f64(bf(Y)).reshape(r // 32, 32, m)
    amax = np.abs(b).max(1)
    byte = np.clip(np.where(amax > 0, np.frexp(amax)[1] - 1 + 127 - 7, 1), 1, 254)
    codes = (b * np.exp2(127.0 - byte)[:, None, :]).reshape(r, m).astype(np.float32).astype(ml_dtypes.float8_e4m3fn).view(np.uint8)
    words = codes.reshape(r // 512, 128, 4, m).transpose(0, 1, 3, 2)
    return np.ascontiguousarray(words), np.ascontiguousarray(byte.astype(np.uint8).reshape(r // 512, 16, m))


K, T, J, R, V, N, C = 1024, 1024, 256, 512, 512, 512, 1024


def setup_inputs():
    n = np.random.standard_normal
    idx = np.random.permutation(T)[:J]
    idx2 = np.random.permutation(V)[:J]
    idx3 = np.random.permutation(V)[:J]
    idx4 = np.random.permutation(C)[:J]
    fk = mx_kscale(K)
    fr = mx_kscale(R)
    wp = pack_weight(n((K, R)) * 1 / np.sqrt(K) * fk[:, None] * fr, "e5m2")
    return {
        "xf": (n((K, T))).astype(np.float32),
        "ow": (n((K, J)) * 0.7).astype(np.float32),
        "fk": (np.random.uniform(0.5, 2.0, (K, 1)) / fk[:, None]).astype(np.float32),
        "w_words": wp[0],
        "w_scales": wp[1],
        "tb": (n((R, V)) * 0.7 * fr[:, None]).astype(np.float32),
        "wb": (n((R, N)) * 1 / np.sqrt(R) / fr[:, None]).astype(np.float32),
        "old": (1.0 * n((N, C))).astype(np.float32),
        "offs": striped(idx),
        "offs2": striped(idx2),
        "offs3": striped(idx3),
        "offs4": striped(idx4),
    }


def reference(xf, ow, fk, w_words, w_scales, tb, wb, old, offs, offs2, offs3, offs4):
    idx = unstriped(offs)
    idx2 = unstriped(offs2)
    idx3 = unstriped(offs3)
    idx4 = unstriped(offs4)
    wu = unpack_weight(w_words, w_scales, "e5m2")
    u = (f64(xf)[:, idx] - f64(ow)) * f64(fk)
    uq = mxq(u, 0, "e4m3")
    a = wu.T @ uq
    hid = np.maximum(a + f64(tb)[:, idx2] - f64(tb)[:, idx3], 0.0)
    wbq = mxq(f64(wb), 0, "e4m3")
    hidq = mxq(hid, 0, "e5m2")
    p = wbq.T @ hidq
    pp = np.zeros((N, C))
    pp[:, idx4] = p
    y = pp + 0.5 * f64(old)
    words, scales = planes(y)
    return y, words, scales

@@ -1,0 +1,241 @@
+from contextlib import ExitStack
+
+import concourse.mybir as mybir
+
+K, T, J, R, V, N, C = 1024, 1024, 256, 512, 512, 512, 1024
+FLOPS = 2 * K * R * J + 2 * R * N * J
+
+F32 = mybir.dt.float32
+BF16 = mybir.dt.bfloat16
+I32 = mybir.dt.int32
+U32 = mybir.dt.uint32
+U16 = mybir.dt.uint16
+U8 = mybir.dt.uint8
+E4M3 = mybir.dt.float8_e4m3fn_x4
+E5M2 = mybir.dt.float8_e5m2_x4
+ALU = mybir.AluOpType
+COPY = mybir.ActivationFunctionType.Copy
+
+P = 128
+PACK = 4
+PASSES = K // (P * PACK)
+HALF = J // 2
+LIST_COLS = J // 16
+HALF_COLS = LIST_COLS // 2
+SCALAR_CHUNKS = ((0, 256), (256, 256), (512, 128))
+VECTOR_CHUNKS = ((640, 256), (896, 128))
+LAST_ADDS = ((0, 256), (256, 384), (640, 384))
+
+
+def tile_list_offsetpicks_tworeach_scattered_pl_kernel(
+    tc, xf, ow, fk, w_words, w_scales, tb, wb, old, offs, offs2, offs3, offs4, out_0, out_1, out_2
+):
+    nc = tc.nc
+
+    def dealt(rows):
+        return rows.rearrange("(p t) c -> p t c", t=PACK)
+
+    def half(h):
+        return slice(h * HALF, (h + 1) * HALF)
+
+    def half_list(h):
+        return slice(h * HALF_COLS, (h + 1) * HALF_COLS)
+
+    with ExitStack() as ctx:
+        sb = ctx.enter_context(tc.tile_pool(name="sb", bufs=1))
+        ps = ctx.enter_context(tc.psum_pool(name="ps", bufs=1))
+
+        idx = sb.tile([P, LIST_COLS], U16, name="idx")
+        idx2 = sb.tile([P, LIST_COLS], U16, name="idx2")
+        idx3 = sb.tile([P, LIST_COLS], U16, name="idx3")
+        idx4 = sb.tile([P, LIST_COLS], U16, name="idx4")
+        tb_sb = [sb.tile([P, V], F32, name=f"tb{t}") for t in range(PACK)]
+        xf_sb = [[sb.tile([P, T], F32, name=f"xf{z}_{t}") for t in range(PACK)] for z in range(PASSES)]
+        ow_sb = [sb.tile([P, PACK, J], F32, name=f"ow{z}") for z in range(PASSES)]
+        fk_sb = sb.tile([P, PASSES, PACK], F32, name="fk_sb")
+        w_raw = sb.tile([P, PASSES, R], U32, name="w_raw")
+        ws_raw = sb.tile([P, PASSES, R], U8, name="ws_raw")
+        wb_sb = [sb.tile([P, PACK, N // 2], F32, name=f"wb{h}") for h in range(2)]
+        old_sb = [sb.tile([P, C], F32, name=f"old{t}") for t in range(PACK)]
+        pages = [sb.tile([P, C], F32, name=f"page{t}") for t in range(PACK)]
+
+        nc.gpsimd.memset(ws_raw[:].rearrange("p z r -> p (z r)").bitcast(I32), 0)
+        for t in range(PACK):
+            nc.vector.memset(pages[t][:], 0.0)
+
+        tb_rows = dealt(tb)
+        nc.sync.dma_start(out=tb_sb[0][:], in_=tb_rows[:, 0, :])
+        nc.sync.dma_start(idx3[:], offs3)
+        nc.sync.dma_start(out=tb_sb[1][:], in_=tb_rows[:, 1, :])
+        nc.sync.dma_start(idx2[:], offs2)
+        for t in range(2, PACK):
+            nc.sync.dma_start(out=tb_sb[t][:], in_=tb_rows[:, t, :])
+        for z in range(PASSES):
+            k_rows = slice(z * P * PACK, (z + 1) * P * PACK)
+            nc.sync.dma_start(out=ow_sb[z][:], in_=dealt(ow[k_rows, :]))
+            if z == 0:
+                nc.sync.dma_start(idx[:], offs)
+            for t in range(PACK):
+                nc.sync.dma_start(out=xf_sb[z][t][:], in_=dealt(xf[k_rows, :])[:, t, :])
+                if z == 0:
+                    if t == 0:
+                        nc.sync.dma_start(out=fk_sb[:], in_=fk.rearrange("(z p t) o -> p z (t o)", z=PASSES, t=PACK))
+                    nc.sync.dma_start(
+                        out=ws_raw[32 * t : 32 * t + 4, :, :].bitcast(I32),
+                        in_=w_scales[:, 4 * t : 4 * t + 4, :].rearrange("z r c -> r z c").bitcast(I32),
+                    )
+            if z == 0:
+                nc.sync.dma_start(
+                    out=w_raw[:].bitcast(I32), in_=w_words.rearrange("z p c b -> p z (c b)").bitcast(I32)
+                )
+        for h in range(2):
+            nc.sync.dma_start(out=wb_sb[h][:], in_=dealt(wb)[:, :, h * (N // 2) : (h + 1) * (N // 2)])
+        nc.sync.dma_start(idx4[:], offs4)
+        for t in range(PACK):
+            nc.sync.dma_start(out=old_sb[t][:], in_=dealt(old)[:, t, :])
+
+        taken = sb.tile([P, PACK, J], F32, name="taken")
+        shift = sb.tile([P, PACK, J], F32, name="shift")
+        for t in range(PACK):
+            nc.scalar.activation(taken[:, t, :], tb_sb[t][:].indirect(idx3[:]), COPY)
+            nc.vector.tensor_tensor(shift[:, t, :], tb_sb[t][:].indirect(idx2[:]), taken[:, t, :], ALU.subtract)
+
+        diff = [sb.tile([P, PACK, J], F32, name=f"diff{z}") for z in range(PASSES)]
+        u_bf = [sb.tile([P, J, PACK], BF16, name=f"u_bf{z}", align_bytes=64) for z in range(PASSES)]
+        u_codes = [sb.tile([P, J], U32, name=f"u_codes{z}", align_bytes=64) for z in range(PASSES)]
+        u_scales = [sb.tile([P, J], U8, name=f"u_scales{z}", align_bytes=64) for z in range(PASSES)]
+        w_codes = sb.tile([P, PASSES, R], U32, name="w_codes", align_bytes=64)
+        w_sc = sb.tile([P, PASSES, R], U8, name="w_sc", align_bytes=64)
+        a_ps = [ps.tile([P, PACK, HALF], F32, name=f"a_ps{h}") for h in range(2)]
+        p_ps = [ps.tile([P, PACK, HALF], F32, name=f"p_ps{h}") for h in range(2)]
+
+        def u_plane(z, t, cols, list_cols):
+            nc.vector.tensor_tensor(
+                diff[z][:, t, cols], xf_sb[z][t][:].indirect(idx[:, list_cols]), ow_sb[z][:, t, cols], ALU.subtract
+            )
+            nc.scalar.activation(u_bf[z][:, cols, t], diff[z][:, t, cols], COPY, scale=fk_sb[:, z, t : t + 1])
+
+        def quantise(codes, scales, values, fmt):
+            nc.vector.quantize_mx(
+                out=codes.bitcast(fmt), scales=scales, in_=values.rearrange("p c t -> p (c t)")
+            )
+
+        def first_product(z, h):
+            for t in range(PACK):
+                cols = slice(t * P, (t + 1) * P)
+                nc.tensor.matmul_mx(
+                    out=a_ps[h][:, t, :],
+                    lhsT=w_codes[:, z, cols].bitcast(E5M2),
+                    lhsT_scale=w_sc[:, z, cols],
+                    rhs=u_codes[z][:, half(h)].bitcast(E4M3),
+                    rhs_scale=u_scales[z][:, half(h)],
+                    start=(z == 0 and t == 0),
+                    stop=(z == PASSES - 1 and t == PACK - 1),
+                )
+
+        whole = slice(0, J)
+        whole_list = slice(0, LIST_COLS)
+        for t in range(PACK):
+            u_plane(0, t, whole, whole_list)
+        quantise(u_codes[0][:], u_scales[0][:], u_bf[0][:], E4M3)
+        for z in range(PASSES):
+            nc.vector.tensor_copy(
+                out=w_sc[:, z, :].rearrange("p (t m) -> p t m", t=PACK),
+                in_=ws_raw[:, z, :].rearrange("p (m t) -> p t m", t=PACK),
+            )
+            nc.vector.tensor_copy(
+                out=w_codes[:, z, :].rearrange("p (t b i) -> p b t i", t=PACK, i=4),
+                in_=w_raw[:, z, :].rearrange("p (b i t) -> p b t i", t=PACK, i=4),
+            )
+        for h in range(2):
+            first_product(0, h)
+        for t in range(PACK - 1):
+            u_plane(1, t, whole, whole_list)
+        for h in range(2):
+            u_plane(1, PACK - 1, half(h), half_list(h))
+        for h in range(2):
+            quantise(u_codes[1][:, half(h)], u_scales[1][:, half(h)], u_bf[1][:, half(h), :], E4M3)
+            first_product(1, h)
+
+        wb_bf = sb.tile([P, PACK, P, PACK], BF16, name="wb_bf", align_bytes=64)
+        wb_codes = sb.tile([P, N], U32, name="wb_codes", align_bytes=64)
+        wb_scales = sb.tile([P, N], U8, name="wb_scales", align_bytes=64)
+        for h in range(2):
+            nc.scalar.copy(
+                out=wb_bf[:, :, h * 64 : (h + 1) * 64, :].rearrange("p t m j -> p m j t"),
+                in_=wb_sb[h][:].rearrange("p j (m t) -> p m j t", t=PACK),
+            )
+
+        pre = [sb.tile([P, PACK, HALF], F32, name=f"pre{h}") for h in range(2)]
+        hid_bf = [sb.tile([P, HALF, PACK], BF16, name=f"hid_bf{h}", align_bytes=64) for h in range(2)]
+        hid_codes = [sb.tile([P, HALF], U32, name=f"hid_codes{h}", align_bytes=64) for h in range(2)]
+        hid_scales = [sb.tile([P, HALF], U8, name=f"hid_scales{h}", align_bytes=64) for h in range(2)]
+        for h in range(2):
+            nc.vector.tensor_tensor(pre[h][:], a_ps[h][:], shift[:, :, half(h)], ALU.add)
+        for h in range(2):
+            nc.vector.tensor_scalar(
+                hid_bf[h][:].rearrange("p (c i) t -> p c t i", i=4),
+                pre[h][:].rearrange("p t (c i) -> p c t i", i=4),
+                0.0,
+                None,
+                ALU.max,
+            )
+        quantise(hid_codes[0][:], hid_scales[0][:], hid_bf[0][:], E5M2)
+        quantise(wb_codes[:], wb_scales[:], wb_bf[:].rearrange("p t m j -> p (t m) j"), E4M3)
+        quantise(hid_codes[1][:], hid_scales[1][:], hid_bf[1][:], E5M2)
+
+        p_sb = [sb.tile([P, PACK, HALF], F32, name=f"p_sb{h}") for h in range(2)]
+        for h in range(2):
+            for t in range(PACK):
+                cols = slice(t * P, (t + 1) * P)
+                nc.tensor.matmul_mx(
+                    out=p_ps[h][:, t, :],
+                    lhsT=wb_codes[:, cols].bitcast(E4M3),
+                    lhsT_scale=wb_scales[:, cols],
+                    rhs=hid_codes[h][:].bitcast(E5M2),
+                    rhs_scale=hid_scales[h][:],
+                    start=True,
+                    stop=True,
+                )
+        nc.scalar.copy(out=p_sb[0][:], in_=p_ps[0][:])
+        nc.vector.tensor_copy(pages[0][:].indirect(idx4[:, half_list(0)]), p_sb[0][:, 0, :])
+        nc.vector.tensor_copy(out=p_sb[1][:], in_=p_ps[1][:])
+        nc.vector.tensor_copy(pages[0][:].indirect(idx4[:, half_list(1)]), p_sb[1][:, 0, :])
+        for t in range(1, PACK):
+            for h in range(2):
+                nc.scalar.activation(pages[t][:].indirect(idx4[:, half_list(h)]), p_sb[h][:, t, :], COPY)
+
+        y = sb.tile([P, PACK, C], F32, name="y")
+        y_bf = sb.tile([P, C, PACK], BF16, name="y_bf", align_bytes=64)
+        y_codes = sb.tile([P, C], U32, name="y_codes", align_bytes=64)
+        y_scales = sb.tile([P, C], U8, name="y_scales", align_bytes=64)
+        y_rows = dealt(out_0)
+        for t in range(PACK):
+            for c0, width in LAST_ADDS if t == PACK - 1 else ((0, C),):
+                cols = slice(c0, c0 + width)
+                nc.vector.scalar_tensor_tensor(
+                    y[:, t, cols], old_sb[t][:, cols], 0.5, pages[t][:, cols], ALU.mult, ALU.add
+                )
+            nc.sync.dma_start(out=y_rows[:, t, :], in_=y[:, t, :])
+
+        def rounded(cols):
+            return (
+                y_bf[:, cols, :].rearrange("p (c i) t -> p c t i", i=4),
+                y[:, :, cols].rearrange("p t (c i) -> p c t i", i=4),
+            )
+
+        for c0, width in SCALAR_CHUNKS:
+            nc.scalar.copy(*rounded(slice(c0, c0 + width)))
+        for c0, width in VECTOR_CHUNKS:
+            nc.vector.tensor_copy(*rounded(slice(c0, c0 + width)))
+        words_out = out_1[0].rearrange("p c b -> p (c b)").bitcast(I32)
+        for c0, width in (SCALAR_CHUNKS[0], VECTOR_CHUNKS[0], SCALAR_CHUNKS[1], VECTOR_CHUNKS[1], SCALAR_CHUNKS[2]):
+            cols = slice(c0, c0 + width)
+            quantise(y_codes[:, cols], y_scales[:, cols], y_bf[:, cols, :], E4M3)
+            nc.sync.dma_start(out=words_out[:, cols], in_=y_codes[:, cols].bitcast(I32))
+        for q in range(4):
+            queue = nc.scalar if q % 2 else nc.sync
+            queue.dma_start(
+                out=out_2[0, 4 * q : 4 * q + 4, :].bitcast(I32),
+                in_=y_scales[32 * q : 32 * q + 4, :].bitcast(I32),
+            )

@@ -15,6 +15,7 @@ E4M3 = mybir.dt.float8_e4m3fn_x4
 E5M2 = mybir.dt.float8_e5m2_x4
 ALU = mybir.AluOpType
 COPY = mybir.ActivationFunctionType.Copy
+RELU = mybir.ActivationFunctionType.Relu
 
 P = 128
 PACK = 4
@@ -22,9 +23,11 @@ PASSES = K // (P * PACK)
 HALF = J // 2
 LIST_COLS = J // 16
 HALF_COLS = LIST_COLS // 2
-SCALAR_CHUNKS = ((0, 256), (256, 256), (512, 128))
-VECTOR_CHUNKS = ((640, 256), (896, 128))
-LAST_ADDS = ((0, 256), (256, 384), (640, 384))
+SCALAR_CHUNKS = ((0, 128), (128, 256), (384, 128), (512, 64))
+VECTOR_CHUNKS = ((576, 448),)
+LAST_ADDS = ((0, 128), (576, 448), (128, 448))
+QUANT_CHUNKS = ((0, 128), (640, 384), (128, 256), (384, 128), (512, 128))
+CODE_STORES = {640: (640, 384), 128: (0, 384), 512: (384, 256)}
 
 
 def tile_list_offsetpicks_tworeach_scattered_pl_kernel(
@@ -55,7 +58,7 @@ def tile_list_offsetpicks_tworeach_scattered_pl_kernel(
         fk_sb = sb.tile([P, PASSES, PACK], F32, name="fk_sb")
         w_raw = sb.tile([P, PASSES, R], U32, name="w_raw")
         ws_raw = sb.tile([P, PASSES, R], U8, name="ws_raw")
-        wb_sb = [sb.tile([P, PACK, N // 2], F32, name=f"wb{h}") for h in range(2)]
+        wb_sb = [sb.tile([P, PACK, N // 2], F32, name=f"wb{h}", align_bytes=64) for h in range(2)]
         old_sb = [sb.tile([P, C], F32, name=f"old{t}") for t in range(PACK)]
         pages = [sb.tile([P, C], F32, name=f"page{t}") for t in range(PACK)]
 
@@ -66,54 +69,71 @@ def tile_list_offsetpicks_tworeach_scattered_pl_kernel(
         tb_rows = dealt(tb)
         nc.sync.dma_start(out=tb_sb[0][:], in_=tb_rows[:, 0, :])
         nc.sync.dma_start(idx3[:], offs3)
-        nc.sync.dma_start(out=tb_sb[1][:], in_=tb_rows[:, 1, :])
+        for q in range(4):
+            nc.sync.dma_start(
+                out=ws_raw[32 * q : 32 * q + 4, :, :].bitcast(I32),
+                in_=w_scales[:, 4 * q : 4 * q + 4, :].rearrange("z r c -> r z c").bitcast(I32),
+            )
+        nc.sync.dma_start(out=w_raw[:].bitcast(I32), in_=w_words.rearrange("z p c b -> p z (c b)").bitcast(I32))
         nc.sync.dma_start(idx2[:], offs2)
-        for t in range(2, PACK):
+        for t in range(1, PACK - 1):
             nc.sync.dma_start(out=tb_sb[t][:], in_=tb_rows[:, t, :])
+        nc.sync.dma_start(idx[:], offs)
         for z in range(PASSES):
             k_rows = slice(z * P * PACK, (z + 1) * P * PACK)
             nc.sync.dma_start(out=ow_sb[z][:], in_=dealt(ow[k_rows, :]))
-            if z == 0:
-                nc.sync.dma_start(idx[:], offs)
             for t in range(PACK):
                 nc.sync.dma_start(out=xf_sb[z][t][:], in_=dealt(xf[k_rows, :])[:, t, :])
-                if z == 0:
-                    if t == 0:
-                        nc.sync.dma_start(out=fk_sb[:], in_=fk.rearrange("(z p t) o -> p z (t o)", z=PASSES, t=PACK))
-                    nc.sync.dma_start(
-                        out=ws_raw[32 * t : 32 * t + 4, :, :].bitcast(I32),
-                        in_=w_scales[:, 4 * t : 4 * t + 4, :].rearrange("z r c -> r z c").bitcast(I32),
-                    )
-            if z == 0:
-                nc.sync.dma_start(
-                    out=w_raw[:].bitcast(I32), in_=w_words.rearrange("z p c b -> p z (c b)").bitcast(I32)
-                )
+                if z == 0 and t == 0:
+                    nc.sync.dma_start(out=fk_sb[:], in_=fk.rearrange("(z p t) o -> p z (t o)", z=PASSES, t=PACK))
+        nc.sync.dma_start(out=tb_sb[PACK - 1][:], in_=tb_rows[:, PACK - 1, :])
         for h in range(2):
             nc.sync.dma_start(out=wb_sb[h][:], in_=dealt(wb)[:, :, h * (N // 2) : (h + 1) * (N // 2)])
         nc.sync.dma_start(idx4[:], offs4)
         for t in range(PACK):
             nc.sync.dma_start(out=old_sb[t][:], in_=dealt(old)[:, t, :])
 
+        w_codes = sb.tile([P, PASSES, R], U32, name="w_codes", align_bytes=64)
+        w_sc = sb.tile([P, PASSES, R], U8, name="w_sc", align_bytes=64)
+        for z in range(PASSES):
+            nc.vector.tensor_copy(
+                out=w_sc[:, z, :].rearrange("p (t m) -> p t m", t=PACK),
+                in_=ws_raw[:, z, :].rearrange("p (m t) -> p t m", t=PACK),
+            )
+        for z in range(PASSES):
+            nc.vector.tensor_copy(
+                out=w_codes[:, z, :].rearrange("p (t b i) -> p b t i", t=PACK, i=4),
+                in_=w_raw[:, z, :].rearrange("p (b i t) -> p b t i", t=PACK, i=4),
+            )
+
+
         taken = sb.tile([P, PACK, J], F32, name="taken")
         shift = sb.tile([P, PACK, J], F32, name="shift")
-        for t in range(PACK):
+
+        def shift_plane(t):
             nc.scalar.activation(taken[:, t, :], tb_sb[t][:].indirect(idx3[:]), COPY)
             nc.vector.tensor_tensor(shift[:, t, :], tb_sb[t][:].indirect(idx2[:]), taken[:, t, :], ALU.subtract)
+
+        for t in range(PACK - 1):
+            shift_plane(t)
 
         diff = [sb.tile([P, PACK, J], F32, name=f"diff{z}") for z in range(PASSES)]
         u_bf = [sb.tile([P, J, PACK], BF16, name=f"u_bf{z}", align_bytes=64) for z in range(PASSES)]
         u_codes = [sb.tile([P, J], U32, name=f"u_codes{z}", align_bytes=64) for z in range(PASSES)]
         u_scales = [sb.tile([P, J], U8, name=f"u_scales{z}", align_bytes=64) for z in range(PASSES)]
-        w_codes = sb.tile([P, PASSES, R], U32, name="w_codes", align_bytes=64)
-        w_sc = sb.tile([P, PASSES, R], U8, name="w_sc", align_bytes=64)
         a_ps = [ps.tile([P, PACK, HALF], F32, name=f"a_ps{h}") for h in range(2)]
-        p_ps = [ps.tile([P, PACK, HALF], F32, name=f"p_ps{h}") for h in range(2)]
+        p_ps = [ps.tile([P, J], F32, name=f"p_ps{t}") for t in range(PACK)]
 
         def u_plane(z, t, cols, list_cols):
             nc.vector.tensor_tensor(
                 diff[z][:, t, cols], xf_sb[z][t][:].indirect(idx[:, list_cols]), ow_sb[z][:, t, cols], ALU.subtract
             )
-            nc.scalar.activation(u_bf[z][:, cols, t], diff[z][:, t, cols], COPY, scale=fk_sb[:, z, t : t + 1])
+            if z == PASSES - 1 and t >= 2:
+                nc.vector.tensor_scalar(
+                    u_bf[z][:, cols, t], diff[z][:, t, cols], fk_sb[:, z, t : t + 1], None, ALU.mult
+                )
+            else:
+                nc.scalar.activation(u_bf[z][:, cols, t], diff[z][:, t, cols], COPY, scale=fk_sb[:, z, t : t + 1])
 
         def quantise(codes, scales, values, fmt):
             nc.vector.quantize_mx(
@@ -138,15 +158,6 @@ def tile_list_offsetpicks_tworeach_scattered_pl_kernel(
         for t in range(PACK):
             u_plane(0, t, whole, whole_list)
         quantise(u_codes[0][:], u_scales[0][:], u_bf[0][:], E4M3)
-        for z in range(PASSES):
-            nc.vector.tensor_copy(
-                out=w_sc[:, z, :].rearrange("p (t m) -> p t m", t=PACK),
-                in_=ws_raw[:, z, :].rearrange("p (m t) -> p t m", t=PACK),
-            )
-            nc.vector.tensor_copy(
-                out=w_codes[:, z, :].rearrange("p (t b i) -> p b t i", t=PACK, i=4),
-                in_=w_raw[:, z, :].rearrange("p (b i t) -> p b t i", t=PACK, i=4),
-            )
         for h in range(2):
             first_product(0, h)
         for t in range(PACK - 1):
@@ -156,6 +167,7 @@ def tile_list_offsetpicks_tworeach_scattered_pl_kernel(
         for h in range(2):
             quantise(u_codes[1][:, half(h)], u_scales[1][:, half(h)], u_bf[1][:, half(h), :], E4M3)
             first_product(1, h)
+        shift_plane(PACK - 1)
 
         wb_bf = sb.tile([P, PACK, P, PACK], BF16, name="wb_bf", align_bytes=64)
         wb_codes = sb.tile([P, N], U32, name="wb_codes", align_bytes=64)
@@ -167,29 +179,35 @@ def tile_list_offsetpicks_tworeach_scattered_pl_kernel(
             )
 
         pre = [sb.tile([P, PACK, HALF], F32, name=f"pre{h}") for h in range(2)]
-        hid_bf = [sb.tile([P, HALF, PACK], BF16, name=f"hid_bf{h}", align_bytes=64) for h in range(2)]
-        hid_codes = [sb.tile([P, HALF], U32, name=f"hid_codes{h}", align_bytes=64) for h in range(2)]
+        hid_bf = [
+            sb.tile([P, HALF, PACK], BF16, name="hid_bf0", align_bytes=64),
+            sb.tile([P, HALF, PACK], BF16, name="hid_bf1", tag="wb1", align_bytes=64),
+        ]
+        hid_codes = [
+            sb.tile([P, HALF], U32, name="hid_codes0", align_bytes=64),
+            sb.tile([P, HALF], U32, name="hid_codes1", tag="wb_bf", align_bytes=64),
+        ]
         hid_scales = [sb.tile([P, HALF], U8, name=f"hid_scales{h}", align_bytes=64) for h in range(2)]
         for h in range(2):
             nc.vector.tensor_tensor(pre[h][:], a_ps[h][:], shift[:, :, half(h)], ALU.add)
-        for h in range(2):
-            nc.vector.tensor_scalar(
+        def hid_views(h):
+            return (
                 hid_bf[h][:].rearrange("p (c i) t -> p c t i", i=4),
                 pre[h][:].rearrange("p t (c i) -> p c t i", i=4),
-                0.0,
-                None,
-                ALU.max,
             )
-        quantise(hid_codes[0][:], hid_scales[0][:], hid_bf[0][:], E5M2)
-        quantise(wb_codes[:], wb_scales[:], wb_bf[:].rearrange("p t m j -> p (t m) j"), E4M3)
-        quantise(hid_codes[1][:], hid_scales[1][:], hid_bf[1][:], E5M2)
 
-        p_sb = [sb.tile([P, PACK, HALF], F32, name=f"p_sb{h}") for h in range(2)]
+        nc.vector.tensor_scalar(*hid_views(0), 0.0, None, ALU.max)
+        nc.scalar.activation(*hid_views(1), RELU)
+        quantise(wb_codes[:], wb_scales[:], wb_bf[:].rearrange("p t m j -> p (t m) j"), E4M3)
         for h in range(2):
-            for t in range(PACK):
+            quantise(hid_codes[h][:], hid_scales[h][:], hid_bf[h][:], E5M2)
+
+        p_sb = [sb.tile([P, J], F32, name=f"p_sb{t}") for t in range(PACK)]
+        for h in range(2):
+            for t in (1, 0, 2, 3):
                 cols = slice(t * P, (t + 1) * P)
                 nc.tensor.matmul_mx(
-                    out=p_ps[h][:, t, :],
+                    out=p_ps[t][:, half(h)],
                     lhsT=wb_codes[:, cols].bitcast(E4M3),
                     lhsT_scale=wb_scales[:, cols],
                     rhs=hid_codes[h][:].bitcast(E5M2),
@@ -197,13 +215,14 @@ def tile_list_offsetpicks_tworeach_scattered_pl_kernel(
                     start=True,
                     stop=True,
                 )
-        nc.scalar.copy(out=p_sb[0][:], in_=p_ps[0][:])
-        nc.vector.tensor_copy(pages[0][:].indirect(idx4[:, half_list(0)]), p_sb[0][:, 0, :])
-        nc.vector.tensor_copy(out=p_sb[1][:], in_=p_ps[1][:])
-        nc.vector.tensor_copy(pages[0][:].indirect(idx4[:, half_list(1)]), p_sb[1][:, 0, :])
-        for t in range(1, PACK):
-            for h in range(2):
-                nc.scalar.activation(pages[t][:].indirect(idx4[:, half_list(h)]), p_sb[h][:, t, :], COPY)
+        nc.scalar.copy(out=p_sb[1][:], in_=p_ps[1][:])
+        nc.vector.tensor_copy(out=p_sb[0][:], in_=p_ps[0][:])
+        nc.scalar.copy(out=p_sb[2][:], in_=p_ps[2][:])
+        nc.vector.tensor_copy(out=p_sb[3][:], in_=p_ps[3][:])
+        nc.vector.tensor_copy(pages[0][:].indirect(idx4[:]), p_sb[0][:])
+        nc.scalar.activation(pages[1][:].indirect(idx4[:]), p_sb[1][:], COPY)
+        nc.scalar.activation(pages[2][:].indirect(idx4[:]), p_sb[2][:], COPY)
+        nc.scalar.activation(pages[3][:].indirect(idx4[:]), p_sb[3][:], COPY)
 
         y = sb.tile([P, PACK, C], F32, name="y")
         y_bf = sb.tile([P, C, PACK], BF16, name="y_bf", align_bytes=64)
@@ -229,10 +248,13 @@ def tile_list_offsetpicks_tworeach_scattered_pl_kernel(
         for c0, width in VECTOR_CHUNKS:
             nc.vector.tensor_copy(*rounded(slice(c0, c0 + width)))
         words_out = out_1[0].rearrange("p c b -> p (c b)").bitcast(I32)
-        for c0, width in (SCALAR_CHUNKS[0], VECTOR_CHUNKS[0], SCALAR_CHUNKS[1], VECTOR_CHUNKS[1], SCALAR_CHUNKS[2]):
+        for c0, width in QUANT_CHUNKS:
             cols = slice(c0, c0 + width)
             quantise(y_codes[:, cols], y_scales[:, cols], y_bf[:, cols, :], E4M3)
-            nc.sync.dma_start(out=words_out[:, cols], in_=y_codes[:, cols].bitcast(I32))
+            if c0 in CODE_STORES:
+                s0, s_width = CODE_STORES[c0]
+                cols = slice(s0, s0 + s_width)
+                nc.sync.dma_start(out=words_out[:, cols], in_=y_codes[:, cols].bitcast(I32))
         for q in range(4):
             queue = nc.scalar if q % 2 else nc.sync
             queue.dma_start(

@@ -23,9 +23,9 @@ PASSES = K // (P * PACK)
 HALF = J // 2
 LIST_COLS = J // 16
 HALF_COLS = LIST_COLS // 2
-SCALAR_CHUNKS = ((0, 128), (128, 256), (384, 128), (512, 64))
-VECTOR_CHUNKS = ((576, 448),)
-LAST_ADDS = ((0, 128), (576, 448), (128, 448))
+SCALAR_CHUNKS = ((0, 128), (128, 256), (384, 128), (512, 128))
+VECTOR_CHUNKS = ((640, 384),)
+LAST_ADDS = ((0, 128), (128, 512), (640, 384))
 QUANT_CHUNKS = ((0, 128), (640, 384), (128, 256), (384, 128), (512, 128))
 CODE_STORES = {640: (640, 384), 128: (0, 384), 512: (384, 256)}
 
@@ -67,25 +67,44 @@ def tile_list_offsetpicks_tworeach_scattered_pl_kernel(
             nc.vector.memset(pages[t][:], 0.0)
 
         tb_rows = dealt(tb)
-        nc.sync.dma_start(out=tb_sb[0][:], in_=tb_rows[:, 0, :])
-        nc.sync.dma_start(idx3[:], offs3)
-        for q in range(4):
+
+        def k_rows(z):
+            return slice(z * P * PACK, (z + 1) * P * PACK)
+
+        def load_tb(t):
+            nc.sync.dma_start(out=tb_sb[t][:], in_=tb_rows[:, t, :])
+
+        def load_ow(z):
+            nc.sync.dma_start(out=ow_sb[z][:], in_=dealt(ow[k_rows(z), :]))
+
+        def load_xf(z, t):
+            nc.sync.dma_start(out=xf_sb[z][t][:], in_=dealt(xf[k_rows(z), :])[:, t, :])
+
+        def load_w_scales(q):
             nc.sync.dma_start(
                 out=ws_raw[32 * q : 32 * q + 4, :, :].bitcast(I32),
                 in_=w_scales[:, 4 * q : 4 * q + 4, :].rearrange("z r c -> r z c").bitcast(I32),
             )
+
+        load_tb(0)
+        nc.sync.dma_start(idx3[:], offs3)
+        load_tb(1)
+        load_tb(2)
         nc.sync.dma_start(out=w_raw[:].bitcast(I32), in_=w_words.rearrange("z p c b -> p z (c b)").bitcast(I32))
+        load_w_scales(0)
+        load_ow(0)
+        for q in range(1, 4):
+            load_w_scales(q)
         nc.sync.dma_start(idx2[:], offs2)
-        for t in range(1, PACK - 1):
-            nc.sync.dma_start(out=tb_sb[t][:], in_=tb_rows[:, t, :])
+        load_xf(0, 0)
         nc.sync.dma_start(idx[:], offs)
-        for z in range(PASSES):
-            k_rows = slice(z * P * PACK, (z + 1) * P * PACK)
-            nc.sync.dma_start(out=ow_sb[z][:], in_=dealt(ow[k_rows, :]))
-            for t in range(PACK):
-                nc.sync.dma_start(out=xf_sb[z][t][:], in_=dealt(xf[k_rows, :])[:, t, :])
-                if z == 0 and t == 0:
-                    nc.sync.dma_start(out=fk_sb[:], in_=fk.rearrange("(z p t) o -> p z (t o)", z=PASSES, t=PACK))
+        load_xf(0, 1)
+        nc.sync.dma_start(out=fk_sb[:], in_=fk.rearrange("(z p t) o -> p z (t o)", z=PASSES, t=PACK))
+        load_xf(0, 2)
+        load_xf(0, 3)
+        load_ow(1)
+        for t in range(PACK):
+            load_xf(1, t)
         nc.sync.dma_start(out=tb_sb[PACK - 1][:], in_=tb_rows[:, PACK - 1, :])
         for h in range(2):
             nc.sync.dma_start(out=wb_sb[h][:], in_=dealt(wb)[:, :, h * (N // 2) : (h + 1) * (N // 2)])

@@ -19,15 +19,25 @@ RELU = mybir.ActivationFunctionType.Relu
 
 P = 128
 PACK = 4
+LAST = PACK - 1
 PASSES = K // (P * PACK)
-HALF = J // 2
+QUADRANTS = 4
+RUN = 4
+HALVES = 2
+HALF = J // HALVES
 LIST_COLS = J // 16
-HALF_COLS = LIST_COLS // 2
-SCALAR_CHUNKS = ((0, 128), (128, 256), (384, 128), (512, 128))
-VECTOR_CHUNKS = ((640, 384),)
-LAST_ADDS = ((0, 128), (128, 512), (640, 384))
-QUANT_CHUNKS = ((0, 128), (640, 384), (128, 256), (384, 128), (512, 128))
-CODE_STORES = {640: (640, 384), 128: (0, 384), 512: (384, 256)}
+WB_HALF = P // HALVES
+
+SPLIT = 640
+SCALAR_ROUNDS = ((0, 128), (128, 256), (384, 128), (512, 128))
+LAST_PLANE_ADDS = ((0, 128), (128, SPLIT - 128), (SPLIT, C - SPLIT))
+QUANTISED = (
+    (SCALAR_ROUNDS[0], None),
+    ((SPLIT, C - SPLIT), (SPLIT, C - SPLIT)),
+    (SCALAR_ROUNDS[1], (0, 384)),
+    (SCALAR_ROUNDS[2], None),
+    (SCALAR_ROUNDS[3], (384, SPLIT - 384)),
+)
 
 
 def tile_list_offsetpicks_tworeach_scattered_pl_kernel(
@@ -38,11 +48,26 @@ def tile_list_offsetpicks_tworeach_scattered_pl_kernel(
     def dealt(rows):
         return rows.rearrange("(p t) c -> p t c", t=PACK)
 
+    def k_rows(z):
+        return slice(z * P * PACK, (z + 1) * P * PACK)
+
     def half(h):
         return slice(h * HALF, (h + 1) * HALF)
 
     def half_list(h):
-        return slice(h * HALF_COLS, (h + 1) * HALF_COLS)
+        return slice(h * LIST_COLS // HALVES, (h + 1) * LIST_COLS // HALVES)
+
+    def span(first, width):
+        return slice(first, first + width)
+
+    def interleaved(out, planes):
+        return (
+            out.rearrange("p (c i) t -> p c t i", i=RUN),
+            planes.rearrange("p t (c i) -> p c t i", i=RUN),
+        )
+
+    def quantise(codes, scales, values, fmt):
+        nc.vector.quantize_mx(out=codes.bitcast(fmt), scales=scales, in_=values.rearrange("p c t -> p (c t)"))
 
     with ExitStack() as ctx:
         sb = ctx.enter_context(tc.tile_pool(name="sb", bufs=1))
@@ -56,23 +81,18 @@ def tile_list_offsetpicks_tworeach_scattered_pl_kernel(
         xf_sb = [[sb.tile([P, T], F32, name=f"xf{z}_{t}") for t in range(PACK)] for z in range(PASSES)]
         ow_sb = [sb.tile([P, PACK, J], F32, name=f"ow{z}") for z in range(PASSES)]
         fk_sb = sb.tile([P, PASSES, PACK], F32, name="fk_sb")
-        w_raw = sb.tile([P, PASSES, R], U32, name="w_raw")
-        ws_raw = sb.tile([P, PASSES, R], U8, name="ws_raw")
-        wb_sb = [sb.tile([P, PACK, N // 2], F32, name=f"wb{h}", align_bytes=64) for h in range(2)]
+        w_words_raw = sb.tile([P, PASSES, R], U32, name="w_words_raw")
+        w_scales_raw = sb.tile([P, PASSES, R], U8, name="w_scales_raw")
+        wb_sb = [sb.tile([P, PACK, N // HALVES], F32, name=f"wb{h}", align_bytes=64) for h in range(HALVES)]
         old_sb = [sb.tile([P, C], F32, name=f"old{t}") for t in range(PACK)]
         pages = [sb.tile([P, C], F32, name=f"page{t}") for t in range(PACK)]
 
-        nc.gpsimd.memset(ws_raw[:].rearrange("p z r -> p (z r)").bitcast(I32), 0)
+        nc.gpsimd.memset(w_scales_raw[:].rearrange("p z r -> p (z r)").bitcast(I32), 0)
         for t in range(PACK):
             nc.vector.memset(pages[t][:], 0.0)
 
-        tb_rows = dealt(tb)
-
-        def k_rows(z):
-            return slice(z * P * PACK, (z + 1) * P * PACK)
-
         def load_tb(t):
-            nc.sync.dma_start(out=tb_sb[t][:], in_=tb_rows[:, t, :])
+            nc.sync.dma_start(out=tb_sb[t][:], in_=dealt(tb)[:, t, :])
 
         def load_ow(z):
             nc.sync.dma_start(out=ow_sb[z][:], in_=dealt(ow[k_rows(z), :]))
@@ -82,7 +102,7 @@ def tile_list_offsetpicks_tworeach_scattered_pl_kernel(
 
         def load_w_scales(q):
             nc.sync.dma_start(
-                out=ws_raw[32 * q : 32 * q + 4, :, :].bitcast(I32),
+                out=w_scales_raw[32 * q : 32 * q + 4, :, :].bitcast(I32),
                 in_=w_scales[:, 4 * q : 4 * q + 4, :].rearrange("z r c -> r z c").bitcast(I32),
             )
 
@@ -90,10 +110,12 @@ def tile_list_offsetpicks_tworeach_scattered_pl_kernel(
         nc.sync.dma_start(idx3[:], offs3)
         load_tb(1)
         load_tb(2)
-        nc.sync.dma_start(out=w_raw[:].bitcast(I32), in_=w_words.rearrange("z p c b -> p z (c b)").bitcast(I32))
+        nc.sync.dma_start(
+            out=w_words_raw[:].bitcast(I32), in_=w_words.rearrange("z p c b -> p z (c b)").bitcast(I32)
+        )
         load_w_scales(0)
         load_ow(0)
-        for q in range(1, 4):
+        for q in range(1, QUADRANTS):
             load_w_scales(q)
         nc.sync.dma_start(idx2[:], offs2)
         load_xf(0, 0)
@@ -105,99 +127,102 @@ def tile_list_offsetpicks_tworeach_scattered_pl_kernel(
         load_ow(1)
         for t in range(PACK):
             load_xf(1, t)
-        nc.sync.dma_start(out=tb_sb[PACK - 1][:], in_=tb_rows[:, PACK - 1, :])
-        for h in range(2):
-            nc.sync.dma_start(out=wb_sb[h][:], in_=dealt(wb)[:, :, h * (N // 2) : (h + 1) * (N // 2)])
+        load_tb(LAST)
+        for h in range(HALVES):
+            nc.sync.dma_start(out=wb_sb[h][:], in_=dealt(wb)[:, :, span(h * N // HALVES, N // HALVES)])
         nc.sync.dma_start(idx4[:], offs4)
         for t in range(PACK):
             nc.sync.dma_start(out=old_sb[t][:], in_=dealt(old)[:, t, :])
 
         w_codes = sb.tile([P, PASSES, R], U32, name="w_codes", align_bytes=64)
-        w_sc = sb.tile([P, PASSES, R], U8, name="w_sc", align_bytes=64)
+        w_scale_plane = sb.tile([P, PASSES, R], U8, name="w_scale_plane", align_bytes=64)
         for z in range(PASSES):
             nc.vector.tensor_copy(
-                out=w_sc[:, z, :].rearrange("p (t m) -> p t m", t=PACK),
-                in_=ws_raw[:, z, :].rearrange("p (m t) -> p t m", t=PACK),
+                out=w_scale_plane[:, z, :].rearrange("p (t m) -> p t m", t=PACK),
+                in_=w_scales_raw[:, z, :].rearrange("p (m t) -> p t m", t=PACK),
             )
         for z in range(PASSES):
             nc.vector.tensor_copy(
-                out=w_codes[:, z, :].rearrange("p (t b i) -> p b t i", t=PACK, i=4),
-                in_=w_raw[:, z, :].rearrange("p (b i t) -> p b t i", t=PACK, i=4),
+                out=w_codes[:, z, :].rearrange("p (t b i) -> p b t i", t=PACK, i=RUN),
+                in_=w_words_raw[:, z, :].rearrange("p (b i t) -> p b t i", t=PACK, i=RUN),
             )
 
-
-        taken = sb.tile([P, PACK, J], F32, name="taken")
+        taken_off = sb.tile([P, PACK, J], F32, name="taken_off")
         shift = sb.tile([P, PACK, J], F32, name="shift")
 
         def shift_plane(t):
-            nc.scalar.activation(taken[:, t, :], tb_sb[t][:].indirect(idx3[:]), COPY)
-            nc.vector.tensor_tensor(shift[:, t, :], tb_sb[t][:].indirect(idx2[:]), taken[:, t, :], ALU.subtract)
+            nc.scalar.activation(taken_off[:, t, :], tb_sb[t][:].indirect(idx3[:]), COPY)
+            nc.vector.tensor_tensor(shift[:, t, :], tb_sb[t][:].indirect(idx2[:]), taken_off[:, t, :], ALU.subtract)
 
-        for t in range(PACK - 1):
+        for t in range(LAST):
             shift_plane(t)
 
         diff = [sb.tile([P, PACK, J], F32, name=f"diff{z}") for z in range(PASSES)]
         u_bf = [sb.tile([P, J, PACK], BF16, name=f"u_bf{z}", align_bytes=64) for z in range(PASSES)]
         u_codes = [sb.tile([P, J], U32, name=f"u_codes{z}", align_bytes=64) for z in range(PASSES)]
         u_scales = [sb.tile([P, J], U8, name=f"u_scales{z}", align_bytes=64) for z in range(PASSES)]
-        a_ps = [ps.tile([P, PACK, HALF], F32, name=f"a_ps{h}") for h in range(2)]
+        a_ps = [ps.tile([P, PACK, HALF], F32, name=f"a_ps{h}") for h in range(HALVES)]
         p_ps = [ps.tile([P, J], F32, name=f"p_ps{t}") for t in range(PACK)]
 
-        def u_plane(z, t, cols, list_cols):
+        def gather_diff(z, t, slots, list_cols):
             nc.vector.tensor_tensor(
-                diff[z][:, t, cols], xf_sb[z][t][:].indirect(idx[:, list_cols]), ow_sb[z][:, t, cols], ALU.subtract
+                diff[z][:, t, slots], xf_sb[z][t][:].indirect(idx[:, list_cols]), ow_sb[z][:, t, slots], ALU.subtract
             )
-            if z == PASSES - 1 and t >= 2:
-                nc.vector.tensor_scalar(
-                    u_bf[z][:, cols, t], diff[z][:, t, cols], fk_sb[:, z, t : t + 1], None, ALU.mult
-                )
-            else:
-                nc.scalar.activation(u_bf[z][:, cols, t], diff[z][:, t, cols], COPY, scale=fk_sb[:, z, t : t + 1])
 
-        def quantise(codes, scales, values, fmt):
-            nc.vector.quantize_mx(
-                out=codes.bitcast(fmt), scales=scales, in_=values.rearrange("p c t -> p (c t)")
-            )
+        def scale_on_scalar(z, t):
+            nc.scalar.activation(u_bf[z][:, :, t], diff[z][:, t, :], COPY, scale=fk_sb[:, z, t : t + 1])
+
+        def scale_on_vector(z, t, slots):
+            nc.vector.tensor_scalar(u_bf[z][:, slots, t], diff[z][:, t, slots], fk_sb[:, z, t : t + 1], None, ALU.mult)
 
         def first_product(z, h):
             for t in range(PACK):
-                cols = slice(t * P, (t + 1) * P)
+                cols = span(t * P, P)
                 nc.tensor.matmul_mx(
                     out=a_ps[h][:, t, :],
                     lhsT=w_codes[:, z, cols].bitcast(E5M2),
-                    lhsT_scale=w_sc[:, z, cols],
+                    lhsT_scale=w_scale_plane[:, z, cols],
                     rhs=u_codes[z][:, half(h)].bitcast(E4M3),
                     rhs_scale=u_scales[z][:, half(h)],
                     start=(z == 0 and t == 0),
-                    stop=(z == PASSES - 1 and t == PACK - 1),
+                    stop=(z == PASSES - 1 and t == LAST),
                 )
 
-        whole = slice(0, J)
-        whole_list = slice(0, LIST_COLS)
+        all_slots = slice(0, J)
+        all_list_cols = slice(0, LIST_COLS)
         for t in range(PACK):
-            u_plane(0, t, whole, whole_list)
+            gather_diff(0, t, all_slots, all_list_cols)
+            scale_on_scalar(0, t)
         quantise(u_codes[0][:], u_scales[0][:], u_bf[0][:], E4M3)
-        for h in range(2):
+        for h in range(HALVES):
             first_product(0, h)
-        for t in range(PACK - 1):
-            u_plane(1, t, whole, whole_list)
-        for h in range(2):
-            u_plane(1, PACK - 1, half(h), half_list(h))
-        for h in range(2):
+
+        for t in range(2):
+            gather_diff(1, t, all_slots, all_list_cols)
+            scale_on_scalar(1, t)
+        gather_diff(1, 2, all_slots, all_list_cols)
+        scale_on_vector(1, 2, all_slots)
+        picked = sb.tile([P, HALF], F32, name="picked")
+        nc.scalar.activation(picked[:], xf_sb[1][LAST][:].indirect(idx[:, half_list(1)]), COPY)
+        gather_diff(1, LAST, half(0), half_list(0))
+        nc.vector.tensor_tensor(diff[1][:, LAST, half(1)], picked[:], ow_sb[1][:, LAST, half(1)], ALU.subtract)
+        for h in range(HALVES):
+            scale_on_vector(1, LAST, half(h))
+        for h in range(HALVES):
             quantise(u_codes[1][:, half(h)], u_scales[1][:, half(h)], u_bf[1][:, half(h), :], E4M3)
             first_product(1, h)
-        shift_plane(PACK - 1)
+        shift_plane(LAST)
 
         wb_bf = sb.tile([P, PACK, P, PACK], BF16, name="wb_bf", align_bytes=64)
         wb_codes = sb.tile([P, N], U32, name="wb_codes", align_bytes=64)
         wb_scales = sb.tile([P, N], U8, name="wb_scales", align_bytes=64)
-        for h in range(2):
+        for h in range(HALVES):
             nc.scalar.copy(
-                out=wb_bf[:, :, h * 64 : (h + 1) * 64, :].rearrange("p t m j -> p m j t"),
+                out=wb_bf[:, :, span(h * WB_HALF, WB_HALF), :].rearrange("p t m j -> p m j t"),
                 in_=wb_sb[h][:].rearrange("p j (m t) -> p m j t", t=PACK),
             )
 
-        pre = [sb.tile([P, PACK, HALF], F32, name=f"pre{h}") for h in range(2)]
+        pre = [sb.tile([P, PACK, HALF], F32, name=f"pre{h}") for h in range(HALVES)]
         hid_bf = [
             sb.tile([P, HALF, PACK], BF16, name="hid_bf0", align_bytes=64),
             sb.tile([P, HALF, PACK], BF16, name="hid_bf1", tag="wb1", align_bytes=64),
@@ -206,25 +231,22 @@ def tile_list_offsetpicks_tworeach_scattered_pl_kernel(
             sb.tile([P, HALF], U32, name="hid_codes0", align_bytes=64),
             sb.tile([P, HALF], U32, name="hid_codes1", tag="wb_bf", align_bytes=64),
         ]
-        hid_scales = [sb.tile([P, HALF], U8, name=f"hid_scales{h}", align_bytes=64) for h in range(2)]
-        for h in range(2):
+        hid_scales = [sb.tile([P, HALF], U8, name=f"hid_scales{h}", align_bytes=64) for h in range(HALVES)]
+        for h in range(HALVES):
             nc.vector.tensor_tensor(pre[h][:], a_ps[h][:], shift[:, :, half(h)], ALU.add)
-        def hid_views(h):
-            return (
-                hid_bf[h][:].rearrange("p (c i) t -> p c t i", i=4),
-                pre[h][:].rearrange("p t (c i) -> p c t i", i=4),
-            )
-
-        nc.vector.tensor_scalar(*hid_views(0), 0.0, None, ALU.max)
-        nc.scalar.activation(*hid_views(1), RELU)
-        quantise(wb_codes[:], wb_scales[:], wb_bf[:].rearrange("p t m j -> p (t m) j"), E4M3)
-        for h in range(2):
+        nc.vector.tensor_scalar(*interleaved(hid_bf[0][:], pre[0][:]), 0.0, None, ALU.max)
+        nc.scalar.activation(*interleaved(hid_bf[1][:], pre[1][:]), RELU)
+        for h in range(HALVES):
+            for t in range(PACK):
+                cols = span(t * P + h * WB_HALF, WB_HALF)
+                quantise(wb_codes[:, cols], wb_scales[:, cols], wb_bf[:, t, span(h * WB_HALF, WB_HALF), :], E4M3)
+        for h in range(HALVES):
             quantise(hid_codes[h][:], hid_scales[h][:], hid_bf[h][:], E5M2)
 
         p_sb = [sb.tile([P, J], F32, name=f"p_sb{t}") for t in range(PACK)]
-        for h in range(2):
+        for h in range(HALVES):
             for t in (1, 0, 2, 3):
-                cols = slice(t * P, (t + 1) * P)
+                cols = span(t * P, P)
                 nc.tensor.matmul_mx(
                     out=p_ps[t][:, half(h)],
                     lhsT=wb_codes[:, cols].bitcast(E4M3),
@@ -239,42 +261,34 @@ def tile_list_offsetpicks_tworeach_scattered_pl_kernel(
         nc.scalar.copy(out=p_sb[2][:], in_=p_ps[2][:])
         nc.vector.tensor_copy(out=p_sb[3][:], in_=p_ps[3][:])
         nc.vector.tensor_copy(pages[0][:].indirect(idx4[:]), p_sb[0][:])
-        nc.scalar.activation(pages[1][:].indirect(idx4[:]), p_sb[1][:], COPY)
-        nc.scalar.activation(pages[2][:].indirect(idx4[:]), p_sb[2][:], COPY)
-        nc.scalar.activation(pages[3][:].indirect(idx4[:]), p_sb[3][:], COPY)
+        for t in range(1, PACK):
+            nc.scalar.activation(pages[t][:].indirect(idx4[:]), p_sb[t][:], COPY)
 
         y = sb.tile([P, PACK, C], F32, name="y")
         y_bf = sb.tile([P, C, PACK], BF16, name="y_bf", align_bytes=64)
         y_codes = sb.tile([P, C], U32, name="y_codes", align_bytes=64)
         y_scales = sb.tile([P, C], U8, name="y_scales", align_bytes=64)
-        y_rows = dealt(out_0)
         for t in range(PACK):
-            for c0, width in LAST_ADDS if t == PACK - 1 else ((0, C),):
-                cols = slice(c0, c0 + width)
+            for piece in LAST_PLANE_ADDS if t == LAST else ((0, C),):
+                cols = span(*piece)
                 nc.vector.scalar_tensor_tensor(
                     y[:, t, cols], old_sb[t][:, cols], 0.5, pages[t][:, cols], ALU.mult, ALU.add
                 )
-            nc.sync.dma_start(out=y_rows[:, t, :], in_=y[:, t, :])
+            nc.sync.dma_start(out=dealt(out_0)[:, t, :], in_=y[:, t, :])
 
-        def rounded(cols):
-            return (
-                y_bf[:, cols, :].rearrange("p (c i) t -> p c t i", i=4),
-                y[:, :, cols].rearrange("p t (c i) -> p c t i", i=4),
-            )
+        for piece in SCALAR_ROUNDS:
+            cols = span(*piece)
+            nc.scalar.copy(*interleaved(y_bf[:, cols, :], y[:, :, cols]))
+        nc.vector.tensor_copy(*interleaved(y_bf[:, SPLIT:C, :], y[:, :, SPLIT:C]))
 
-        for c0, width in SCALAR_CHUNKS:
-            nc.scalar.copy(*rounded(slice(c0, c0 + width)))
-        for c0, width in VECTOR_CHUNKS:
-            nc.vector.tensor_copy(*rounded(slice(c0, c0 + width)))
         words_out = out_1[0].rearrange("p c b -> p (c b)").bitcast(I32)
-        for c0, width in QUANT_CHUNKS:
-            cols = slice(c0, c0 + width)
+        for piece, stored in QUANTISED:
+            cols = span(*piece)
             quantise(y_codes[:, cols], y_scales[:, cols], y_bf[:, cols, :], E4M3)
-            if c0 in CODE_STORES:
-                s0, s_width = CODE_STORES[c0]
-                cols = slice(s0, s0 + s_width)
+            if stored is not None:
+                cols = span(*stored)
                 nc.sync.dma_start(out=words_out[:, cols], in_=y_codes[:, cols].bitcast(I32))
-        for q in range(4):
+        for q in range(QUADRANTS):
             queue = nc.scalar if q % 2 else nc.sync
             queue.dma_start(
                 out=out_2[0, 4 * q : 4 * q + 4, :].bitcast(I32),

from contextlib import ExitStack

import concourse.mybir as mybir

K, T, J, R, V, N, C = 1024, 1024, 256, 512, 512, 512, 1024
FLOPS = 2 * K * R * J + 2 * R * N * J

F32 = mybir.dt.float32
BF16 = mybir.dt.bfloat16
I32 = mybir.dt.int32
U32 = mybir.dt.uint32
U16 = mybir.dt.uint16
U8 = mybir.dt.uint8
E4M3 = mybir.dt.float8_e4m3fn_x4
E5M2 = mybir.dt.float8_e5m2_x4
ALU = mybir.AluOpType
COPY = mybir.ActivationFunctionType.Copy
RELU = mybir.ActivationFunctionType.Relu

P = 128
PACK = 4
LAST = PACK - 1
PASSES = K // (P * PACK)
QUADRANTS = 4
RUN = 4
HALVES = 2
HALF = J // HALVES
LIST_COLS = J // 16
WB_HALF = P // HALVES

SPLIT = 640
SCALAR_ROUNDS = ((0, 128), (128, 256), (384, 128), (512, 128))
LAST_PLANE_ADDS = ((0, 128), (128, SPLIT - 128), (SPLIT, C - SPLIT))
QUANTISED = (
    (SCALAR_ROUNDS[0], None),
    ((SPLIT, C - SPLIT), (SPLIT, C - SPLIT)),
    (SCALAR_ROUNDS[1], (0, 384)),
    (SCALAR_ROUNDS[2], None),
    (SCALAR_ROUNDS[3], (384, SPLIT - 384)),
)


def tile_list_offsetpicks_tworeach_scattered_pl_kernel(
    tc, xf, ow, fk, w_words, w_scales, tb, wb, old, offs, offs2, offs3, offs4, out_0, out_1, out_2
):
    nc = tc.nc

    def dealt(rows):
        return rows.rearrange("(p t) c -> p t c", t=PACK)

    def k_rows(z):
        return slice(z * P * PACK, (z + 1) * P * PACK)

    def half(h):
        return slice(h * HALF, (h + 1) * HALF)

    def half_list(h):
        return slice(h * LIST_COLS // HALVES, (h + 1) * LIST_COLS // HALVES)

    def span(first, width):
        return slice(first, first + width)

    def interleaved(out, planes):
        return (
            out.rearrange("p (c i) t -> p c t i", i=RUN),
            planes.rearrange("p t (c i) -> p c t i", i=RUN),
        )

    def quantise(codes, scales, values, fmt):
        nc.vector.quantize_mx(out=codes.bitcast(fmt), scales=scales, in_=values.rearrange("p c t -> p (c t)"))

    with ExitStack() as ctx:
        sb = ctx.enter_context(tc.tile_pool(name="sb", bufs=1))
        ps = ctx.enter_context(tc.psum_pool(name="ps", bufs=1))

        idx = sb.tile([P, LIST_COLS], U16, name="idx")
        idx2 = sb.tile([P, LIST_COLS], U16, name="idx2")
        idx3 = sb.tile([P, LIST_COLS], U16, name="idx3")
        idx4 = sb.tile([P, LIST_COLS], U16, name="idx4")
        tb_sb = [sb.tile([P, V], F32, name=f"tb{t}") for t in range(PACK)]
        xf_sb = [[sb.tile([P, T], F32, name=f"xf{z}_{t}") for t in range(PACK)] for z in range(PASSES)]
        ow_sb = [sb.tile([P, PACK, J], F32, name=f"ow{z}") for z in range(PASSES)]
        fk_sb = sb.tile([P, PASSES, PACK], F32, name="fk_sb")
        w_words_raw = sb.tile([P, PASSES, R], U32, name="w_words_raw")
        w_scales_raw = sb.tile([P, PASSES, R], U8, name="w_scales_raw")
        wb_sb = [sb.tile([P, PACK, N // HALVES], F32, name=f"wb{h}", align_bytes=64) for h in range(HALVES)]
        old_sb = [sb.tile([P, C], F32, name=f"old{t}") for t in range(PACK)]
        pages = [sb.tile([P, C], F32, name=f"page{t}") for t in range(PACK)]

        nc.gpsimd.memset(w_scales_raw[:].rearrange("p z r -> p (z r)").bitcast(I32), 0)
        for t in range(PACK):
            nc.vector.memset(pages[t][:], 0.0)

        def load_tb(t):
            nc.sync.dma_start(out=tb_sb[t][:], in_=dealt(tb)[:, t, :])

        def load_ow(z):
            nc.sync.dma_start(out=ow_sb[z][:], in_=dealt(ow[k_rows(z), :]))

        def load_xf(z, t):
            nc.sync.dma_start(out=xf_sb[z][t][:], in_=dealt(xf[k_rows(z), :])[:, t, :])

        def load_w_scales(q):
            nc.sync.dma_start(
                out=w_scales_raw[32 * q : 32 * q + 4, :, :].bitcast(I32),
                in_=w_scales[:, 4 * q : 4 * q + 4, :].rearrange("z r c -> r z c").bitcast(I32),
            )

        load_tb(0)
        nc.sync.dma_start(idx3[:], offs3)
        load_tb(1)
        load_tb(2)
        nc.sync.dma_start(
            out=w_words_raw[:].bitcast(I32), in_=w_words.rearrange("z p c b -> p z (c b)").bitcast(I32)
        )
        load_w_scales(0)
        load_ow(0)
        for q in range(1, QUADRANTS):
            load_w_scales(q)
        nc.sync.dma_start(idx2[:], offs2)
        load_xf(0, 0)
        nc.sync.dma_start(idx[:], offs)
        load_xf(0, 1)
        nc.sync.dma_start(out=fk_sb[:], in_=fk.rearrange("(z p t) o -> p z (t o)", z=PASSES, t=PACK))
        load_xf(0, 2)
        load_xf(0, 3)
        load_ow(1)
        for t in range(PACK):
            load_xf(1, t)
        load_tb(LAST)
        for h in range(HALVES):
            nc.sync.dma_start(out=wb_sb[h][:], in_=dealt(wb)[:, :, span(h * N // HALVES, N // HALVES)])
        nc.sync.dma_start(idx4[:], offs4)
        for t in range(PACK):
            nc.sync.dma_start(out=old_sb[t][:], in_=dealt(old)[:, t, :])

        w_codes = sb.tile([P, PASSES, R], U32, name="w_codes", align_bytes=64)
        w_scale_plane = sb.tile([P, PASSES, R], U8, name="w_scale_plane", align_bytes=64)
        for z in range(PASSES):
            nc.vector.tensor_copy(
                out=w_scale_plane[:, z, :].rearrange("p (t m) -> p t m", t=PACK),
                in_=w_scales_raw[:, z, :].rearrange("p (m t) -> p t m", t=PACK),
            )
        for z in range(PASSES):
            nc.vector.tensor_copy(
                out=w_codes[:, z, :].rearrange("p (t b i) -> p b t i", t=PACK, i=RUN),
                in_=w_words_raw[:, z, :].rearrange("p (b i t) -> p b t i", t=PACK, i=RUN),
            )

        taken_off = sb.tile([P, PACK, J], F32, name="taken_off")
        shift = sb.tile([P, PACK, J], F32, name="shift")

        def shift_plane(t):
            nc.scalar.activation(taken_off[:, t, :], tb_sb[t][:].indirect(idx3[:]), COPY)
            nc.vector.tensor_tensor(shift[:, t, :], tb_sb[t][:].indirect(idx2[:]), taken_off[:, t, :], ALU.subtract)

        for t in range(LAST):
            shift_plane(t)

        diff = [sb.tile([P, PACK, J], F32, name=f"diff{z}") for z in range(PASSES)]
        u_bf = [sb.tile([P, J, PACK], BF16, name=f"u_bf{z}", align_bytes=64) for z in range(PASSES)]
        u_codes = [sb.tile([P, J], U32, name=f"u_codes{z}", align_bytes=64) for z in range(PASSES)]
        u_scales = [sb.tile([P, J], U8, name=f"u_scales{z}", align_bytes=64) for z in range(PASSES)]
        a_ps = [ps.tile([P, PACK, HALF], F32, name=f"a_ps{h}") for h in range(HALVES)]
        p_ps = [ps.tile([P, J], F32, name=f"p_ps{t}") for t in range(PACK)]

        def gather_diff(z, t, slots, list_cols):
            nc.vector.tensor_tensor(
                diff[z][:, t, slots], xf_sb[z][t][:].indirect(idx[:, list_cols]), ow_sb[z][:, t, slots], ALU.subtract
            )

        def scale_on_scalar(z, t):
            nc.scalar.activation(u_bf[z][:, :, t], diff[z][:, t, :], COPY, scale=fk_sb[:, z, t : t + 1])

        def scale_on_vector(z, t, slots):
            nc.vector.tensor_scalar(u_bf[z][:, slots, t], diff[z][:, t, slots], fk_sb[:, z, t : t + 1], None, ALU.mult)

        def first_product(z, h):
            for t in range(PACK):
                cols = span(t * P, P)
                nc.tensor.matmul_mx(
                    out=a_ps[h][:, t, :],
                    lhsT=w_codes[:, z, cols].bitcast(E5M2),
                    lhsT_scale=w_scale_plane[:, z, cols],
                    rhs=u_codes[z][:, half(h)].bitcast(E4M3),
                    rhs_scale=u_scales[z][:, half(h)],
                    start=(z == 0 and t == 0),
                    stop=(z == PASSES - 1 and t == LAST),
                )

        all_slots = slice(0, J)
        all_list_cols = slice(0, LIST_COLS)
        for t in range(PACK):
            gather_diff(0, t, all_slots, all_list_cols)
            scale_on_scalar(0, t)
        quantise(u_codes[0][:], u_scales[0][:], u_bf[0][:], E4M3)
        for h in range(HALVES):
            first_product(0, h)

        for t in range(2):
            gather_diff(1, t, all_slots, all_list_cols)
            scale_on_scalar(1, t)
        gather_diff(1, 2, all_slots, all_list_cols)
        scale_on_vector(1, 2, all_slots)
        picked = sb.tile([P, HALF], F32, name="picked")
        nc.scalar.activation(picked[:], xf_sb[1][LAST][:].indirect(idx[:, half_list(1)]), COPY)
        gather_diff(1, LAST, half(0), half_list(0))
        nc.vector.tensor_tensor(diff[1][:, LAST, half(1)], picked[:], ow_sb[1][:, LAST, half(1)], ALU.subtract)
        for h in range(HALVES):
            scale_on_vector(1, LAST, half(h))
        for h in range(HALVES):
            quantise(u_codes[1][:, half(h)], u_scales[1][:, half(h)], u_bf[1][:, half(h), :], E4M3)
            first_product(1, h)
        shift_plane(LAST)

        wb_bf = sb.tile([P, PACK, P, PACK], BF16, name="wb_bf", align_bytes=64)
        wb_codes = sb.tile([P, N], U32, name="wb_codes", align_bytes=64)
        wb_scales = sb.tile([P, N], U8, name="wb_scales", align_bytes=64)
        for h in range(HALVES):
            nc.scalar.copy(
                out=wb_bf[:, :, span(h * WB_HALF, WB_HALF), :].rearrange("p t m j -> p m j t"),
                in_=wb_sb[h][:].rearrange("p j (m t) -> p m j t", t=PACK),
            )

        pre = [sb.tile([P, PACK, HALF], F32, name=f"pre{h}") for h in range(HALVES)]
        hid_bf = [
            sb.tile([P, HALF, PACK], BF16, name="hid_bf0", align_bytes=64),
            sb.tile([P, HALF, PACK], BF16, name="hid_bf1", tag="wb1", align_bytes=64),
        ]
        hid_codes = [
            sb.tile([P, HALF], U32, name="hid_codes0", align_bytes=64),
            sb.tile([P, HALF], U32, name="hid_codes1", tag="wb_bf", align_bytes=64),
        ]
        hid_scales = [sb.tile([P, HALF], U8, name=f"hid_scales{h}", align_bytes=64) for h in range(HALVES)]
        for h in range(HALVES):
            nc.vector.tensor_tensor(pre[h][:], a_ps[h][:], shift[:, :, half(h)], ALU.add)
        nc.vector.tensor_scalar(*interleaved(hid_bf[0][:], pre[0][:]), 0.0, None, ALU.max)
        nc.scalar.activation(*interleaved(hid_bf[1][:], pre[1][:]), RELU)
        for h in range(HALVES):
            for t in range(PACK):
                cols = span(t * P + h * WB_HALF, WB_HALF)
                quantise(wb_codes[:, cols], wb_scales[:, cols], wb_bf[:, t, span(h * WB_HALF, WB_HALF), :], E4M3)
        for h in range(HALVES):
            quantise(hid_codes[h][:], hid_scales[h][:], hid_bf[h][:], E5M2)

        p_sb = [sb.tile([P, J], F32, name=f"p_sb{t}") for t in range(PACK)]
        for h in range(HALVES):
            for t in (1, 0, 2, 3):
                cols = span(t * P, P)
                nc.tensor.matmul_mx(
                    out=p_ps[t][:, half(h)],
                    lhsT=wb_codes[:, cols].bitcast(E4M3),
                    lhsT_scale=wb_scales[:, cols],
                    rhs=hid_codes[h][:].bitcast(E5M2),
                    rhs_scale=hid_scales[h][:],
                    start=True,
                    stop=True,
                )
        nc.scalar.copy(out=p_sb[1][:], in_=p_ps[1][:])
        nc.vector.tensor_copy(out=p_sb[0][:], in_=p_ps[0][:])
        nc.scalar.copy(out=p_sb[2][:], in_=p_ps[2][:])
        nc.vector.tensor_copy(out=p_sb[3][:], in_=p_ps[3][:])
        nc.vector.tensor_copy(pages[0][:].indirect(idx4[:]), p_sb[0][:])
        for t in range(1, PACK):
            nc.scalar.activation(pages[t][:].indirect(idx4[:]), p_sb[t][:], COPY)

        y = sb.tile([P, PACK, C], F32, name="y")
        y_bf = sb.tile([P, C, PACK], BF16, name="y_bf", align_bytes=64)
        y_codes = sb.tile([P, C], U32, name="y_codes", align_bytes=64)
        y_scales = sb.tile([P, C], U8, name="y_scales", align_bytes=64)
        for t in range(PACK):
            for piece in LAST_PLANE_ADDS if t == LAST else ((0, C),):
                cols = span(*piece)
                nc.vector.scalar_tensor_tensor(
                    y[:, t, cols], old_sb[t][:, cols], 0.5, pages[t][:, cols], ALU.mult, ALU.add
                )
            nc.sync.dma_start(out=dealt(out_0)[:, t, :], in_=y[:, t, :])

        for piece in SCALAR_ROUNDS:
            cols = span(*piece)
            nc.scalar.copy(*interleaved(y_bf[:, cols, :], y[:, :, cols]))
        nc.vector.tensor_copy(*interleaved(y_bf[:, SPLIT:C, :], y[:, :, SPLIT:C]))

        words_out = out_1[0].rearrange("p c b -> p (c b)").bitcast(I32)
        for piece, stored in QUANTISED:
            cols = span(*piece)
            quantise(y_codes[:, cols], y_scales[:, cols], y_bf[:, cols, :], E4M3)
            if stored is not None:
                cols = span(*stored)
                nc.sync.dma_start(out=words_out[:, cols], in_=y_codes[:, cols].bitcast(I32))
        for q in range(QUADRANTS):
            queue = nc.scalar if q % 2 else nc.sync
            queue.dma_start(
                out=out_2[0, 4 * q : 4 * q + 4, :].bitcast(I32),
                in_=y_scales[32 * q : 32 * q + 4, :].bitcast(I32),
            )
